import numpy as np, ml_dtypes
CORES = [24,48,72,152,176,200]
N = 6
import mx_ref
NC, G = 384, 2
C = np.float32(0.023)
CNT = [[0,384,0,0,0,0],[0,0,128,0,256,0],[0,0,256,0,0,128],[256,0,0,128,0,0],[128,0,0,256,0,0],[0,0,0,0,128,256]]
OFF = [[sum(c[:e]) for e in range(N + 1)] for c in CNT]
BF = ml_dtypes.bfloat16
def cut(t, i, w=512):
    return t[:, w * i:w * i + w]
def tile(rs):
    return np.stack(rs, axis=2).reshape(128, -1).astype(BF)
def layer(w, X):
    out = []
    for i in range(G):
        for t in range(len(X)):
            p = mx_ref.matmul(mx_ref.quantize(cut(w, len(X) * i + t)), X[t])
            z = p if t == 0 else z + p
        out.append(z)
    return out
def act(Z):
    return [np.maximum(s * z, 0) * C for z in Z for s in (1, -1)]
def setup_inputs(rng):
    def f(*shape):
        return mx_ref.flush((rng.standard_normal(shape, dtype=np.float32) * np.exp2(rng.integers(-2, 3, shape[:-1] + (1,)))).astype(BF))
    return {"x": f(N, 128, 4 * NC), "w1": f(N, 128, G * 512), "w2": f(N, 128, 512)}
def setup_inputs_blocks(rng):
    d = setup_inputs(rng)
    for k in ("x", "w1", "w2"): d[k] = mx_ref.spread(d[k], rng, 4)
    return d
def setup_inputs_wide(rng):
    d = setup_inputs(rng)
    for k in ("x", "w1", "w2"): d[k] = mx_ref.flush((d[k].astype(np.float32) * np.exp2(rng.integers(-8, 9, (N, 1, 1))).astype(np.float32)).astype(BF))
    return d
def setup_inputs_zeros(rng):
    d = setup_inputs(rng); v = d["x"].reshape(N, 128, -1, 4).copy()
    v[np.broadcast_to((rng.random((N, 1, v.shape[2], 1)) < 0.33), v.shape)] = 0
    d["x"] = v.reshape(d["x"].shape)
    return d
def reference(x, w1, w2):
    y = np.zeros((N, 128, NC), np.float32)
    for e in range(N):
        t = np.concatenate([x[j][:, 4 * OFF[j][e]:4 * OFF[j][e + 1]] for j in range(N)], axis=1)
        p = mx_ref.matmul(mx_ref.quantize(w2[e]), mx_ref.quantize(tile(act(layer(w1[e], [mx_ref.quantize(t)])))))
        c = 0
        for j in range(N):
            a, b = OFF[j][e], OFF[j][e + 1]
            y[j][:, a:b] = p[:, c:c + b - a]; c += b - a
    return {"y": y}

@@ -1,0 +1,214 @@
+import comms_topo
+from concourse.bass import DstId, RemoteDMATransfer
+from concourse.mybir import dt, AluOpType, ActivationFunctionType
+
+NSIM = 256
+NC = 384
+WC = 384
+TW = 128
+CH = 128
+NCH = NC // CH
+NSLOT = 2
+C = 0.023
+
+SCRATCH = {
+    "wt": ("sbuf", [128, 4 * WC], "bfloat16"),
+    "xt": ("sbuf", [128, 4 * NC], "bfloat16"),
+    "wqc": ("sbuf", [128, WC], "float8_e4m3fn_x4"),
+    "wqs": ("sbuf", [128, WC], "uint8"),
+    "xqc": ("sbuf", [128, NC], "float8_e4m3fn_x4"),
+    "xqs": ("sbuf", [128, NC], "uint8"),
+    "rc": ("sbuf", [128, NSLOT * WC], "float8_e4m3fn_x4"),
+    "rs": ("sbuf", [128, NSLOT * WC], "uint8"),
+    "h": ("sbuf", [128, 4 * NC], "bfloat16"),
+    "hqc": ("sbuf", [128, NC], "float8_e4m3fn_x4"),
+    "hqs": ("sbuf", [128, NC], "uint8"),
+    "yo": ("sbuf", [128, NC], "float32"),
+    "ps": ("psum", [128, 512 * 2 * NCH], "float32"),
+}
+SEMAPHORES = (["wload", "xload", "wq", "xq", "hs", "hc", "sent", "st"]
+              + ["wa%d" % s for s in range(NSLOT)]
+              + ["%s%d" % (n, k) for n in ("za", "zb", "act", "hq", "p", "yo") for k in range(NCH)])
+
+
+def _bits(mask):
+    return [i for i in range(mask.bit_length()) if (mask >> i) & 1]
+
+
+def _mk(engines):
+    m = 0
+    for i in engines:
+        m |= 1 << i
+    return m
+
+
+def _plan(T, topo):
+    cores = list(T.cores)
+    cnt = T.tables["CNT"]
+    n = len(cores)
+    users = [[j for j in range(n) if j != e and cnt[j][e] > 0] for e in range(n)]
+    near = [[j for j in users[e] if topo.may_write(cores[e], cores[j])] for e in range(n)]
+    far = [[j for j in users[e] if not topo.may_write(cores[e], cores[j])] for e in range(n)]
+    relays = []
+    for e in range(n):
+        src = cores[e]
+        picked = {}
+        if far[e]:
+            for c in range(NSIM):
+                if (topo.host(c), topo.chip(c)) != (topo.host(src), topo.chip(src)) or c in cores:
+                    continue
+                if all(topo.may_write(c, cores[j]) for j in far[e]):
+                    picked.setdefault(topo.die(c), c)
+        own = topo.die(src)
+        relays.append([picked[d] for d in sorted(picked, key=lambda d: d != own)])
+    return cores, cnt, n, near, far, relays
+
+
+def _send(g, T, topo, core, dst, out_ap, in_ap, sem):
+    rid, pid = topo.addr(dst, core)
+    m = topo.mask(core, dst)
+    g.remote_dma(out_ap=out_ap, in_ap=in_ap, remote_sem=sem, local_sem=T.sem.sent, pid=pid, routing_id=rid,
+                 dma_engine_mask=m)
+    return len(_bits(m))
+
+
+def rank_program(g, core, T, topo):
+    cores, cnt, n, near, far, relays = _plan(T, topo)
+    u8 = dt.uint8
+
+    def slot(j, e):
+        return [k for k in range(n) if k != j and cnt[j][k] > 0].index(e)
+
+    rank = T.rank_of(core)
+
+    if rank is None:
+        for e in range(n):
+            if core not in relays[e]:
+                continue
+            k = len(relays[e])
+            i = relays[e].index(core)
+            a, b = i * (WC // k), (i + 1) * (WC // k)
+            got = len(_bits(topo.mask(cores[e], core))[i::k])
+            sent = 0
+            g.wait_ge(T.sem.hs, got)
+            for j in far[e]:
+                o = slot(j, e) * WC
+                sent += _send(g, T, topo, core, cores[j], T.rs[:, o + a:o + b], T.rs[:, a:b], T.sem["wa%d" % slot(j, e)])
+            g.wait_ge(T.sem.hc, got)
+            for j in far[e]:
+                o = slot(j, e) * WC
+                sent += _send(g, T, topo, core, cores[j], T.rc[:, o + a:o + b].bitcast(u8), T.rc[:, a:b].bitcast(u8),
+                              T.sem["wa%d" % slot(j, e)])
+            g.wait_ge(T.sem.sent, sent)
+        return
+
+    g.sync.dma_start(T.wt[:, 0:8 * TW], T.w1[:, :]).then_inc(T.sem.wload, 16)
+    g.scalar.dma_start(T.wt[:, 8 * TW:12 * TW], T.w2[:, :]).then_inc(T.sem.wload, 16)
+    g.sync.dma_start(T.xt[:, :], T.x[:, :]).then_inc(T.sem.xload, 16)
+
+    g.vector.wait_ge(T.sem.wload, 32)
+    g.vector.quantize_mx(T.wqc[:, :], T.wqs[:, :], T.wt[:, :]).then_inc(T.sem.wq, 1)
+    g.vector.wait_ge(T.sem.xload, 16)
+    g.vector.quantize_mx(T.xqc[:, :], T.xqs[:, :], T.xt[:, :]).then_inc(T.sem.xq, 1)
+
+    sent = 0
+    g.wait_ge(T.sem.wq, 1)
+    if far[rank]:
+        hl = relays[rank]
+        k = len(hl)
+        w = WC // k
+        for codes in (False, True):
+            trs = []
+            for i, hcore in enumerate(hl):
+                engines = _bits(topo.mask(core, hcore))[i::k]
+                rid, pid = topo.addr(hcore, core)
+                a, b = i * w, (i + 1) * w
+                if codes:
+                    src, dst, sem = T.wqc[:, a:b].bitcast(u8), T.rc[:, a:b].bitcast(u8), T.sem.hc
+                else:
+                    src, dst, sem = T.wqs[:, a:b], T.rs[:, a:b], T.sem.hs
+                trs.append(RemoteDMATransfer(dst_ids=[DstId(rid=rid, pnc=pid)], dma_engine_mask=_mk(engines),
+                                             remote_sem=sem, src=src, dst=dst))
+                sent += len(engines)
+            g.remote_dma_fused(trs, local_sem=T.sem.sent)
+    for j in near[rank]:
+        o = slot(j, rank) * WC
+        sem = T.sem["wa%d" % slot(j, rank)]
+        sent += _send(g, T, topo, core, cores[j], T.rs[:, o:o + WC], T.wqs[:, :], sem)
+        sent += _send(g, T, topo, core, cores[j], T.rc[:, o:o + WC].bitcast(u8), T.wqc[:, :].bitcast(u8), sem)
+    g.wait_ge(T.sem.sent, sent)
+
+    classes = {}
+    c0 = 0
+    for e in range(n):
+        m = cnt[rank][e]
+        assert m % CH == 0
+        cls = 0 if e == rank else (1 if rank in near[e] else 2)
+        for q in range(m // CH):
+            classes.setdefault(cls, []).append((c0 + q * CH, e))
+        c0 += m
+    groups = [classes[c] for c in sorted(classes)]
+
+    def weights(e):
+        if e == rank:
+            return T.wqc, T.wqs, 0, T.sem.wq, 1
+        s = slot(rank, e)
+        if rank in near[e]:
+            cntw = 2 * len(_bits(topo.mask(cores[e], core)))
+        else:
+            cntw = sum(2 * len(_bits(topo.mask(hc, core))) for hc in relays[e])
+        return T.rc, T.rs, s * WC, T.sem["wa%d" % s], cntw
+
+    te, ve, se, sy = g.tensor, g.vector, g.scalar, g.sync
+    te.wait_ge(T.sem.xq, 1)
+    waited = set()
+    k0 = 0
+    nst = 0
+    for grp in groups:
+        ks = list(range(k0, k0 + len(grp)))
+        k0 += len(grp)
+        for k, (a, e) in zip(ks, grp):
+            wc, ws, o, sem, cw = weights(e)
+            if e not in waited:
+                te.wait_ge(sem, cw)
+                waited.add(e)
+            for i, nm in enumerate(("za", "zb")):
+                te.matmul_mx(T.ps[:, 512 * (2 * k + i):512 * (2 * k + i) + CH],
+                             wc[:, o + i * TW:o + (i + 1) * TW], ws[:, o + i * TW:o + (i + 1) * TW],
+                             T.xqc[:, a:a + CH], T.xqs[:, a:a + CH], True, True).then_inc(T.sem["%s%d" % (nm, k)], 1)
+        for k, (a, e) in zip(ks, grp):
+            wc, ws, o, sem, cw = weights(e)
+            te.wait_ge(T.sem["hq%d" % k], 1)
+            te.matmul_mx(T.ps[:, 512 * 2 * k:512 * 2 * k + CH],
+                         wc[:, o + 2 * TW:o + 3 * TW], ws[:, o + 2 * TW:o + 3 * TW],
+                         T.hqc[:, a:a + CH], T.hqs[:, a:a + CH], True, True).then_inc(T.sem["p%d" % k], 1)
+
+        def quant(k, a):
+            ve.wait_ge(T.sem["act%d" % k], 4)
+            ve.quantize_mx(T.hqc[:, a:a + CH], T.hqs[:, a:a + CH], T.h[:, 4 * a:4 * (a + CH)]).then_inc(T.sem["hq%d" % k], 1)
+
+        prev = None
+        for k, (a, e) in zip(ks, grp):
+            z = T.ps[:, 512 * 2 * k:512 * 2 * k + CH]
+            ve.wait_ge(T.sem["za%d" % k], 1)
+            ve.tensor_scalar(T.h[:, 4 * a + 0:4 * (a + CH):4], z, C, 0.0, AluOpType.mult, AluOpType.max).then_inc(T.sem["act%d" % k], 1)
+            ve.tensor_scalar(T.h[:, 4 * a + 1:4 * (a + CH):4], z, -C, 0.0, AluOpType.mult, AluOpType.max).then_inc(T.sem["act%d" % k], 1)
+            if prev is not None:
+                quant(*prev)
+            prev = (k, a)
+        quant(*prev)
+
+        for k, (a, e) in zip(ks, grp):
+            z = T.ps[:, 512 * (2 * k + 1):512 * (2 * k + 1) + CH]
+            se.wait_ge(T.sem["zb%d" % k], 1)
+            se.activation(T.h[:, 4 * a + 2:4 * (a + CH):4], z, ActivationFunctionType.Relu, scale=C).then_inc(T.sem["act%d" % k], 1)
+            se.activation(T.h[:, 4 * a + 3:4 * (a + CH):4], z, ActivationFunctionType.Relu, scale=-C).then_inc(T.sem["act%d" % k], 1)
+        for k, (a, e) in zip(ks, grp):
+            se.wait_ge(T.sem["p%d" % k], 1)
+            se.activation(T.yo[:, a:a + CH], T.ps[:, 512 * 2 * k:512 * 2 * k + CH], ActivationFunctionType.Copy).then_inc(T.sem["yo%d" % k], 1)
+
+        for k, (a, e) in zip(ks, grp):
+            sy.wait_ge(T.sem["yo%d" % k], 1)
+            sy.dma_start(T.y[:, a:a + CH], T.yo[:, a:a + CH]).then_inc(T.sem.st, 16)
+            nst += 16
+    sy.wait_ge(T.sem.st, nst)

@@ -4,8 +4,8 @@ from concourse.mybir import dt, AluOpType, ActivationFunctionType
 
 NSIM = 256
 NC = 384
-WC = 384
 TW = 128
+WC = 3 * TW
 CH = 128
 NCH = NC // CH
 NSLOT = 2
@@ -26,8 +26,8 @@ SCRATCH = {
     "yo": ("sbuf", [128, NC], "float32"),
     "ps": ("psum", [128, 512 * 2 * NCH], "float32"),
 }
-SEMAPHORES = (["wload", "xload", "wq", "xq", "hs", "hc", "sent", "st"]
-              + ["wa%d" % s for s in range(NSLOT)]
+SEMAPHORES = (["l2", "l1", "lx", "q2", "q1", "xq", "hw2", "hs1", "hc1", "sent", "st"]
+              + ["%s%d" % (n, s) for n in ("wa", "wb") for s in range(NSLOT)]
               + ["%s%d" % (n, k) for n in ("za", "zb", "act", "hq", "p", "yo") for k in range(NCH)])
 
 
@@ -59,25 +59,35 @@ def _plan(T, topo):
                     continue
                 if all(topo.may_write(c, cores[j]) for j in far[e]):
                     picked.setdefault(topo.die(c), c)
+            assert len(picked) == 2
         own = topo.die(src)
         relays.append([picked[d] for d in sorted(picked, key=lambda d: d != own)])
     return cores, cnt, n, near, far, relays
 
 
-def _send(g, T, topo, core, dst, out_ap, in_ap, sem):
-    rid, pid = topo.addr(dst, core)
-    m = topo.mask(core, dst)
-    g.remote_dma(out_ap=out_ap, in_ap=in_ap, remote_sem=sem, local_sem=T.sem.sent, pid=pid, routing_id=rid,
-                 dma_engine_mask=m)
-    return len(_bits(m))
-
-
 def rank_program(g, core, T, topo):
     cores, cnt, n, near, far, relays = _plan(T, topo)
     u8 = dt.uint8
+    total = [0]
 
     def slot(j, e):
         return [k for k in range(n) if k != j and cnt[j][k] > 0].index(e)
+
+    def width(src, dst):
+        return len(_bits(topo.mask(src, dst)))
+
+    def send(dst, codes, a, b, o, sem):
+        own = T.rank_of(core) is not None
+        if codes:
+            in_ap = (T.wqc if own else T.rc)[:, a:b].bitcast(u8)
+            out_ap = T.rc[:, o + a:o + b].bitcast(u8)
+        else:
+            in_ap = (T.wqs if own else T.rs)[:, a:b]
+            out_ap = T.rs[:, o + a:o + b]
+        rid, pid = topo.addr(dst, core)
+        g.remote_dma(out_ap=out_ap, in_ap=in_ap, remote_sem=sem, local_sem=T.sem.sent, pid=pid, routing_id=rid,
+                     dma_engine_mask=topo.mask(core, dst))
+        total[0] += width(core, dst)
 
     rank = T.rank_of(core)
 
@@ -85,58 +95,59 @@ def rank_program(g, core, T, topo):
         for e in range(n):
             if core not in relays[e]:
                 continue
-            k = len(relays[e])
-            i = relays[e].index(core)
-            a, b = i * (WC // k), (i + 1) * (WC // k)
-            got = len(_bits(topo.mask(cores[e], core))[i::k])
-            sent = 0
-            g.wait_ge(T.sem.hs, got)
-            for j in far[e]:
-                o = slot(j, e) * WC
-                sent += _send(g, T, topo, core, cores[j], T.rs[:, o + a:o + b], T.rs[:, a:b], T.sem["wa%d" % slot(j, e)])
-            g.wait_ge(T.sem.hc, got)
-            for j in far[e]:
-                o = slot(j, e) * WC
-                sent += _send(g, T, topo, core, cores[j], T.rc[:, o + a:o + b].bitcast(u8), T.rc[:, a:b].bitcast(u8),
-                              T.sem["wa%d" % slot(j, e)])
-            g.wait_ge(T.sem.sent, sent)
+            first = relays[e].index(core) == 0
+            src = cores[e]
+            dsts = [(cores[j], slot(j, e) * WC, T.sem["wa%d" % slot(j, e)], T.sem["wb%d" % slot(j, e)]) for j in far[e]]
+            g.wait_ge(T.sem.hw2, width(src, core))
+            for d, o, wa, wb in dsts:
+                send(d, not first, 2 * TW, 3 * TW, o, wb)
+            if first:
+                g.wait_ge(T.sem.hs1, width(src, core))
+                for d, o, wa, wb in dsts:
+                    send(d, False, 0, 2 * TW, o, wa)
+            g.wait_ge(T.sem.hc1, width(src, core) // 2)
+            for d, o, wa, wb in dsts:
+                if first:
+                    send(d, True, 0, TW, o, wa)
+                else:
+                    send(d, True, TW, 2 * TW, o, wa)
+            g.wait_ge(T.sem.sent, total[0])
         return
 
-    g.sync.dma_start(T.wt[:, 0:8 * TW], T.w1[:, :]).then_inc(T.sem.wload, 16)
-    g.scalar.dma_start(T.wt[:, 8 * TW:12 * TW], T.w2[:, :]).then_inc(T.sem.wload, 16)
-    g.sync.dma_start(T.xt[:, :], T.x[:, :]).then_inc(T.sem.xload, 16)
+    g.sync.dma_start(T.wt[:, 8 * TW:12 * TW], T.w2[:, :]).then_inc(T.sem.l2, 16)
+    g.sync.dma_start(T.wt[:, 0:8 * TW], T.w1[:, :]).then_inc(T.sem.l1, 16)
+    g.sync.dma_start(T.xt[:, :], T.x[:, :]).then_inc(T.sem.lx, 16)
 
-    g.vector.wait_ge(T.sem.wload, 32)
-    g.vector.quantize_mx(T.wqc[:, :], T.wqs[:, :], T.wt[:, :]).then_inc(T.sem.wq, 1)
-    g.vector.wait_ge(T.sem.xload, 16)
+    g.vector.wait_ge(T.sem.l2, 16)
+    g.vector.quantize_mx(T.wqc[:, 2 * TW:3 * TW], T.wqs[:, 2 * TW:3 * TW], T.wt[:, 8 * TW:12 * TW]).then_inc(T.sem.q2, 1)
+    g.vector.wait_ge(T.sem.l1, 16)
+    g.vector.quantize_mx(T.wqc[:, 0:2 * TW], T.wqs[:, 0:2 * TW], T.wt[:, 0:8 * TW]).then_inc(T.sem.q1, 1)
+    g.vector.wait_ge(T.sem.lx, 16)
     g.vector.quantize_mx(T.xqc[:, :], T.xqs[:, :], T.xt[:, :]).then_inc(T.sem.xq, 1)
 
-    sent = 0
-    g.wait_ge(T.sem.wq, 1)
+    g.wait_ge(T.sem.q2, 1)
     if far[rank]:
-        hl = relays[rank]
-        k = len(hl)
-        w = WC // k
-        for codes in (False, True):
-            trs = []
-            for i, hcore in enumerate(hl):
-                engines = _bits(topo.mask(core, hcore))[i::k]
-                rid, pid = topo.addr(hcore, core)
-                a, b = i * w, (i + 1) * w
-                if codes:
-                    src, dst, sem = T.wqc[:, a:b].bitcast(u8), T.rc[:, a:b].bitcast(u8), T.sem.hc
-                else:
-                    src, dst, sem = T.wqs[:, a:b], T.rs[:, a:b], T.sem.hs
-                trs.append(RemoteDMATransfer(dst_ids=[DstId(rid=rid, pnc=pid)], dma_engine_mask=_mk(engines),
-                                             remote_sem=sem, src=src, dst=dst))
-                sent += len(engines)
-            g.remote_dma_fused(trs, local_sem=T.sem.sent)
+        ra, rb = relays[rank]
+        send(rb, True, 2 * TW, 3 * TW, 0, T.sem.hw2)
+        send(ra, False, 2 * TW, 3 * TW, 0, T.sem.hw2)
+    g.wait_ge(T.sem.q1, 1)
+    if far[rank]:
+        send(ra, False, 0, 2 * TW, 0, T.sem.hs1)
+        trs = []
+        for i, hcore in enumerate((ra, rb)):
+            engines = _bits(topo.mask(core, hcore))[i::2]
+            rid, pid = topo.addr(hcore, core)
+            trs.append(RemoteDMATransfer(dst_ids=[DstId(rid=rid, pnc=pid)], dma_engine_mask=_mk(engines),
+                                         remote_sem=T.sem.hc1, src=T.wqc[:, i * TW:(i + 1) * TW].bitcast(u8),
+                                         dst=T.rc[:, i * TW:(i + 1) * TW].bitcast(u8)))
+            total[0] += len(engines)
+        g.remote_dma_fused(trs, local_sem=T.sem.sent)
     for j in near[rank]:
         o = slot(j, rank) * WC
         sem = T.sem["wa%d" % slot(j, rank)]
-        sent += _send(g, T, topo, core, cores[j], T.rs[:, o:o + WC], T.wqs[:, :], sem)
-        sent += _send(g, T, topo, core, cores[j], T.rc[:, o:o + WC].bitcast(u8), T.wqc[:, :].bitcast(u8), sem)
-    g.wait_ge(T.sem.sent, sent)
+        send(cores[j], False, 0, WC, o, sem)
+        send(cores[j], True, 0, WC, o, sem)
+    g.wait_ge(T.sem.sent, total[0])
 
     classes = {}
     c0 = 0
@@ -151,33 +162,37 @@ def rank_program(g, core, T, topo):
 
     def weights(e):
         if e == rank:
-            return T.wqc, T.wqs, 0, T.sem.wq, 1
+            return T.wqc, T.wqs, 0, (T.sem.q1, 1), (T.sem.q2, 1)
         s = slot(rank, e)
         if rank in near[e]:
-            cntw = 2 * len(_bits(topo.mask(cores[e], core)))
-        else:
-            cntw = sum(2 * len(_bits(topo.mask(hc, core))) for hc in relays[e])
-        return T.rc, T.rs, s * WC, T.sem["wa%d" % s], cntw
+            return T.rc, T.rs, s * WC, (T.sem["wa%d" % s], 2 * width(cores[e], core)), None
+        ra, rb = relays[e]
+        return (T.rc, T.rs, s * WC, (T.sem["wa%d" % s], 2 * width(ra, core) + width(rb, core)),
+                (T.sem["wb%d" % s], width(ra, core) + width(rb, core)))
 
     te, ve, se, sy = g.tensor, g.vector, g.scalar, g.sync
     te.wait_ge(T.sem.xq, 1)
-    waited = set()
+    waited1, waited2 = set(), set()
     k0 = 0
     nst = 0
     for grp in groups:
         ks = list(range(k0, k0 + len(grp)))
         k0 += len(grp)
         for k, (a, e) in zip(ks, grp):
-            wc, ws, o, sem, cw = weights(e)
-            if e not in waited:
-                te.wait_ge(sem, cw)
-                waited.add(e)
+            wc, ws, o, w1s, w2s = weights(e)
+            if e not in waited1:
+                te.wait_ge(w1s[0], w1s[1])
+                waited1.add(e)
             for i, nm in enumerate(("za", "zb")):
                 te.matmul_mx(T.ps[:, 512 * (2 * k + i):512 * (2 * k + i) + CH],
                              wc[:, o + i * TW:o + (i + 1) * TW], ws[:, o + i * TW:o + (i + 1) * TW],
                              T.xqc[:, a:a + CH], T.xqs[:, a:a + CH], True, True).then_inc(T.sem["%s%d" % (nm, k)], 1)
         for k, (a, e) in zip(ks, grp):
-            wc, ws, o, sem, cw = weights(e)
+            wc, ws, o, w1s, w2s = weights(e)
+            if e not in waited2:
+                if w2s is not None:
+                    te.wait_ge(w2s[0], w2s[1])
+                waited2.add(e)
             te.wait_ge(T.sem["hq%d" % k], 1)
             te.matmul_mx(T.ps[:, 512 * 2 * k:512 * 2 * k + CH],
                          wc[:, o + 2 * TW:o + 3 * TW], ws[:, o + 2 * TW:o + 3 * TW],

@@ -5,7 +5,8 @@ from concourse.mybir import dt, AluOpType, ActivationFunctionType
 NSIM = 256
 NC = 384
 TW = 128
-WC = 3 * TW
+NT = 3
+WC = NT * TW
 CH = 128
 NCH = NC // CH
 NSLOT = 2
@@ -26,9 +27,14 @@ SCRATCH = {
     "yo": ("sbuf", [128, NC], "float32"),
     "ps": ("psum", [128, 512 * 2 * NCH], "float32"),
 }
-SEMAPHORES = (["l2", "l1", "lx", "q2", "q1", "xq", "hw2", "hs1", "hc1", "sent", "st"]
-              + ["%s%d" % (n, s) for n in ("wa", "wb") for s in range(NSLOT)]
-              + ["%s%d" % (n, k) for n in ("za", "zb", "act", "hq", "p", "yo") for k in range(NCH)])
+SEMAPHORES = (["go", "sent", "st"]
+              + ["%s%d" % (n, t) for n in ("l", "q") for t in range(NT)]
+              + ["hp%d" % p for p in range(2 * NT)]
+              + ["w%d_%d" % (t, s) for t in range(NT) for s in range(NSLOT)]
+              + ["%s%d" % (n, k) for n in ("lx", "xq", "za", "zb", "act", "hq", "p", "yo") for k in range(NCH)])
+
+ASSIGN = {2: [0, 1, 1, 0, 0, 1],
+          4: [0, 2, 1, 3, 2, 3]}
 
 
 def _bits(mask):
@@ -47,152 +53,153 @@ def _plan(T, topo):
     cnt = T.tables["CNT"]
     n = len(cores)
     users = [[j for j in range(n) if j != e and cnt[j][e] > 0] for e in range(n)]
-    near = [[j for j in users[e] if topo.may_write(cores[e], cores[j])] for e in range(n)]
-    far = [[j for j in users[e] if not topo.may_write(cores[e], cores[j])] for e in range(n)]
-    relays = []
+    helpers = []
     for e in range(n):
         src = cores[e]
-        picked = {}
-        if far[e]:
-            for c in range(NSIM):
-                if (topo.host(c), topo.chip(c)) != (topo.host(src), topo.chip(src)) or c in cores:
-                    continue
-                if all(topo.may_write(c, cores[j]) for j in far[e]):
-                    picked.setdefault(topo.die(c), c)
-            assert len(picked) == 2
-        own = topo.die(src)
-        relays.append([picked[d] for d in sorted(picked, key=lambda d: d != own)])
-    return cores, cnt, n, near, far, relays
+        by_die = {}
+        for c in range(NSIM):
+            if (topo.host(c), topo.chip(c)) != (topo.host(src), topo.chip(src)) or c in cores:
+                continue
+            if all(topo.may_write(c, cores[j]) for j in users[e]):
+                by_die.setdefault(topo.die(c), []).append(c)
+        dies = sorted(by_die, key=lambda d: d != topo.die(src))
+        hs = []
+        for r in range(len(users[e])):
+            for d in dies:
+                hs.append(by_die[d][r])
+        assert not users[e] or len(hs) in ASSIGN
+        helpers.append(hs)
+    return cores, cnt, n, users, helpers
 
 
 def rank_program(g, core, T, topo):
-    cores, cnt, n, near, far, relays = _plan(T, topo)
+    cores, cnt, n, users, helpers = _plan(T, topo)
     u8 = dt.uint8
     total = [0]
 
     def slot(j, e):
         return [k for k in range(n) if k != j and cnt[j][k] > 0].index(e)
 
-    def width(src, dst):
-        return len(_bits(topo.mask(src, dst)))
+    def engines_to(e, hcore, j):
+        i = users[e].index(j)
+        return _bits(topo.mask(hcore, cores[j]))[i::len(users[e])]
 
-    def send(dst, codes, a, b, o, sem):
-        own = T.rank_of(core) is not None
-        if codes:
-            in_ap = (T.wqc if own else T.rc)[:, a:b].bitcast(u8)
-            out_ap = T.rc[:, o + a:o + b].bitcast(u8)
-        else:
-            in_ap = (T.wqs if own else T.rs)[:, a:b]
-            out_ap = T.rs[:, o + a:o + b]
-        rid, pid = topo.addr(dst, core)
-        g.remote_dma(out_ap=out_ap, in_ap=in_ap, remote_sem=sem, local_sem=T.sem.sent, pid=pid, routing_id=rid,
-                     dma_engine_mask=topo.mask(core, dst))
-        total[0] += width(core, dst)
+    def view(codes_buf, plane_buf, p, o):
+        a = o + (p // 2) * TW
+        if p % 2 == 0:
+            return codes_buf[:, a:a + TW].bitcast(u8)
+        return plane_buf[:, a:a + TW]
 
     rank = T.rank_of(core)
 
     if rank is None:
         for e in range(n):
-            if core not in relays[e]:
+            if core not in helpers[e]:
                 continue
-            first = relays[e].index(core) == 0
-            src = cores[e]
-            dsts = [(cores[j], slot(j, e) * WC, T.sem["wa%d" % slot(j, e)], T.sem["wb%d" % slot(j, e)]) for j in far[e]]
-            g.wait_ge(T.sem.hw2, width(src, core))
-            for d, o, wa, wb in dsts:
-                send(d, not first, 2 * TW, 3 * TW, o, wb)
-            if first:
-                g.wait_ge(T.sem.hs1, width(src, core))
-                for d, o, wa, wb in dsts:
-                    send(d, False, 0, 2 * TW, o, wa)
-            g.wait_ge(T.sem.hc1, width(src, core) // 2)
-            for d, o, wa, wb in dsts:
-                if first:
-                    send(d, True, 0, TW, o, wa)
-                else:
-                    send(d, True, TW, 2 * TW, o, wa)
+            me = helpers[e].index(core)
+            assign = ASSIGN[len(helpers[e])]
+            for p in range(2 * NT):
+                if assign[p] != me:
+                    continue
+                g.wait_ge(T.sem["hp%d" % p], len(_bits(topo.mask(cores[e], core))))
+                trs = []
+                for j in users[e]:
+                    eng = engines_to(e, core, j)
+                    rid, pid = topo.addr(cores[j], core)
+                    trs.append(RemoteDMATransfer(dst_ids=[DstId(rid=rid, pnc=pid)], dma_engine_mask=_mk(eng),
+                                                 remote_sem=T.sem["w%d_%d" % (p // 2, slot(j, e))],
+                                                 src=view(T.rc, T.rs, p, 0), dst=view(T.rc, T.rs, p, slot(j, e) * WC)))
+                    total[0] += len(eng)
+                g.remote_dma_fused(trs, local_sem=T.sem.sent)
             g.wait_ge(T.sem.sent, total[0])
         return
 
-    g.sync.dma_start(T.wt[:, 8 * TW:12 * TW], T.w2[:, :]).then_inc(T.sem.l2, 16)
-    g.sync.dma_start(T.wt[:, 0:8 * TW], T.w1[:, :]).then_inc(T.sem.l1, 16)
-    g.sync.dma_start(T.xt[:, :], T.x[:, :]).then_inc(T.sem.lx, 16)
-
-    g.vector.wait_ge(T.sem.l2, 16)
-    g.vector.quantize_mx(T.wqc[:, 2 * TW:3 * TW], T.wqs[:, 2 * TW:3 * TW], T.wt[:, 8 * TW:12 * TW]).then_inc(T.sem.q2, 1)
-    g.vector.wait_ge(T.sem.l1, 16)
-    g.vector.quantize_mx(T.wqc[:, 0:2 * TW], T.wqs[:, 0:2 * TW], T.wt[:, 0:8 * TW]).then_inc(T.sem.q1, 1)
-    g.vector.wait_ge(T.sem.lx, 16)
-    g.vector.quantize_mx(T.xqc[:, :], T.xqs[:, :], T.xt[:, :]).then_inc(T.sem.xq, 1)
-
-    g.wait_ge(T.sem.q2, 1)
-    if far[rank]:
-        ra, rb = relays[rank]
-        send(rb, True, 2 * TW, 3 * TW, 0, T.sem.hw2)
-        send(ra, False, 2 * TW, 3 * TW, 0, T.sem.hw2)
-    g.wait_ge(T.sem.q1, 1)
-    if far[rank]:
-        send(ra, False, 0, 2 * TW, 0, T.sem.hs1)
-        trs = []
-        for i, hcore in enumerate((ra, rb)):
-            engines = _bits(topo.mask(core, hcore))[i::2]
-            rid, pid = topo.addr(hcore, core)
-            trs.append(RemoteDMATransfer(dst_ids=[DstId(rid=rid, pnc=pid)], dma_engine_mask=_mk(engines),
-                                         remote_sem=T.sem.hc1, src=T.wqc[:, i * TW:(i + 1) * TW].bitcast(u8),
-                                         dst=T.rc[:, i * TW:(i + 1) * TW].bitcast(u8)))
-            total[0] += len(engines)
-        g.remote_dma_fused(trs, local_sem=T.sem.sent)
-    for j in near[rank]:
-        o = slot(j, rank) * WC
-        sem = T.sem["wa%d" % slot(j, rank)]
-        send(cores[j], False, 0, WC, o, sem)
-        send(cores[j], True, 0, WC, o, sem)
-    g.wait_ge(T.sem.sent, total[0])
-
-    classes = {}
+    own, foreign = [], []
     c0 = 0
     for e in range(n):
         m = cnt[rank][e]
         assert m % CH == 0
-        cls = 0 if e == rank else (1 if rank in near[e] else 2)
         for q in range(m // CH):
-            classes.setdefault(cls, []).append((c0 + q * CH, e))
+            (own if e == rank else foreign).append((c0 + q * CH, e))
         c0 += m
-    groups = [classes[c] for c in sorted(classes)]
+    foreign.sort(key=lambda ae: (len(users[ae[1]]), ae[0]))
+    groups = [grp for grp in (own, foreign) if grp]
+    order = own + foreign
+
+    te, ve, se, sy = g.tensor, g.vector, g.scalar, g.sync
+
+    for t in range(NT):
+        src = T.w1[:, 4 * TW * t:4 * TW * (t + 1)] if t < 2 else T.w2[:, :]
+        sy.dma_start(T.wt[:, 4 * TW * t:4 * TW * (t + 1)], src).then_inc(T.sem["l%d" % t], 16)
+    sy.wait_ge(T.sem.go, 1)
+    for k, (a, e) in enumerate(order):
+        sy.dma_start(T.xt[:, 4 * a:4 * (a + CH)], T.x[:, 4 * a:4 * (a + CH)]).then_inc(T.sem["lx%d" % k], 16)
+
+    for t in range(NT):
+        ve.wait_ge(T.sem["l%d" % t], 16)
+        ve.quantize_mx(T.wqc[:, TW * t:TW * (t + 1)], T.wqs[:, TW * t:TW * (t + 1)],
+                       T.wt[:, 4 * TW * t:4 * TW * (t + 1)]).then_inc(T.sem["q%d" % t], 1)
+    for k, (a, e) in enumerate(order):
+        ve.wait_ge(T.sem["lx%d" % k], 16)
+        ve.quantize_mx(T.xqc[:, a:a + CH], T.xqs[:, a:a + CH], T.xt[:, 4 * a:4 * (a + CH)]).then_inc(T.sem["xq%d" % k], 1)
+
+    for t in range(NT):
+        g.wait_ge(T.sem["q%d" % t], 1)
+        if not users[rank]:
+            continue
+        assign = ASSIGN[len(helpers[rank])]
+        for p in (2 * t, 2 * t + 1):
+            hcore = helpers[rank][assign[p]]
+            rid, pid = topo.addr(hcore, core)
+            m = topo.mask(core, hcore)
+            g.remote_dma(out_ap=view(T.rc, T.rs, p, 0), in_ap=view(T.wqc, T.wqs, p, 0), remote_sem=T.sem["hp%d" % p],
+                         local_sem=T.sem.sent, pid=pid, routing_id=rid, dma_engine_mask=m)
+            total[0] += len(_bits(m))
+    g.sem_inc(T.sem.go, 1)
+    g.wait_ge(T.sem.sent, total[0])
 
     def weights(e):
         if e == rank:
-            return T.wqc, T.wqs, 0, (T.sem.q1, 1), (T.sem.q2, 1)
-        s = slot(rank, e)
-        if rank in near[e]:
-            return T.rc, T.rs, s * WC, (T.sem["wa%d" % s], 2 * width(cores[e], core)), None
-        ra, rb = relays[e]
-        return (T.rc, T.rs, s * WC, (T.sem["wa%d" % s], 2 * width(ra, core) + width(rb, core)),
-                (T.sem["wb%d" % s], width(ra, core) + width(rb, core)))
+            return T.wqc, T.wqs, 0
+        return T.rc, T.rs, slot(rank, e) * WC
 
-    te, ve, se, sy = g.tensor, g.vector, g.scalar, g.sync
-    te.wait_ge(T.sem.xq, 1)
-    waited1, waited2 = set(), set()
+    waited = set()
+
+    def wait_tile(e, t):
+        if (e, t) in waited:
+            return
+        waited.add((e, t))
+        if e == rank:
+            te.wait_ge(T.sem["q%d" % t], 1)
+            return
+        assign = ASSIGN[len(helpers[e])]
+        cntr = sum(len(engines_to(e, helpers[e][assign[p]], rank)) for p in (2 * t, 2 * t + 1))
+        te.wait_ge(T.sem["w%d_%d" % (t, slot(rank, e))], cntr)
+
     k0 = 0
     nst = 0
     for grp in groups:
         ks = list(range(k0, k0 + len(grp)))
         k0 += len(grp)
-        for k, (a, e) in zip(ks, grp):
-            wc, ws, o, w1s, w2s = weights(e)
-            if e not in waited1:
-                te.wait_ge(w1s[0], w1s[1])
-                waited1.add(e)
+        experts = []
+        for a, e in grp:
+            if e not in experts:
+                experts.append(e)
+        for e in experts:
+            wc, ws, o = weights(e)
             for i, nm in enumerate(("za", "zb")):
-                te.matmul_mx(T.ps[:, 512 * (2 * k + i):512 * (2 * k + i) + CH],
-                             wc[:, o + i * TW:o + (i + 1) * TW], ws[:, o + i * TW:o + (i + 1) * TW],
-                             T.xqc[:, a:a + CH], T.xqs[:, a:a + CH], True, True).then_inc(T.sem["%s%d" % (nm, k)], 1)
+                wait_tile(e, i)
+                for k, (a, e2) in zip(ks, grp):
+                    if e2 != e:
+                        continue
+                    if i == 0:
+                        te.wait_ge(T.sem["xq%d" % k], 1)
+                    te.matmul_mx(T.ps[:, 512 * (2 * k + i):512 * (2 * k + i) + CH],
+                                 wc[:, o + i * TW:o + (i + 1) * TW], ws[:, o + i * TW:o + (i + 1) * TW],
+                                 T.xqc[:, a:a + CH], T.xqs[:, a:a + CH], True, True).then_inc(T.sem["%s%d" % (nm, k)], 1)
         for k, (a, e) in zip(ks, grp):
-            wc, ws, o, w1s, w2s = weights(e)
-            if e not in waited2:
-                if w2s is not None:
-                    te.wait_ge(w2s[0], w2s[1])
-                waited2.add(e)
+            wc, ws, o = weights(e)
+            wait_tile(e, 2)
             te.wait_ge(T.sem["hq%d" % k], 1)
             te.matmul_mx(T.ps[:, 512 * 2 * k:512 * 2 * k + CH],
                          wc[:, o + 2 * TW:o + 3 * TW], ws[:, o + 2 * TW:o + 3 * TW],

import comms_topo
from concourse.bass import DstId, RemoteDMATransfer
from concourse.mybir import dt, AluOpType, ActivationFunctionType

NSIM = 256
NC = 384
TW = 128
NT = 3
WC = NT * TW
CH = 128
NCH = NC // CH
NSLOT = 2
C = 0.023

SCRATCH = {
    "wt": ("sbuf", [128, 4 * WC], "bfloat16"),
    "xt": ("sbuf", [128, 4 * NC], "bfloat16"),
    "wqc": ("sbuf", [128, WC], "float8_e4m3fn_x4"),
    "wqs": ("sbuf", [128, WC], "uint8"),
    "xqc": ("sbuf", [128, NC], "float8_e4m3fn_x4"),
    "xqs": ("sbuf", [128, NC], "uint8"),
    "rc": ("sbuf", [128, NSLOT * WC], "float8_e4m3fn_x4"),
    "rs": ("sbuf", [128, NSLOT * WC], "uint8"),
    "h": ("sbuf", [128, 4 * NC], "bfloat16"),
    "hqc": ("sbuf", [128, NC], "float8_e4m3fn_x4"),
    "hqs": ("sbuf", [128, NC], "uint8"),
    "yo": ("sbuf", [128, NC], "float32"),
    "ps": ("psum", [128, 512 * 2 * NCH], "float32"),
}
SEMAPHORES = (["go", "sent", "st"]
              + ["%s%d" % (n, t) for n in ("l", "q") for t in range(NT)]
              + ["hp%d" % p for p in range(2 * NT)]
              + ["w%d_%d" % (t, s) for t in range(NT) for s in range(NSLOT)]
              + ["%s%d" % (n, k) for n in ("lx", "xq", "za", "zb", "act", "hq", "p", "yo") for k in range(NCH)])

ASSIGN = {2: [0, 1, 1, 0, 0, 1],
          4: [0, 2, 1, 3, 2, 3]}


def _bits(mask):
    return [i for i in range(mask.bit_length()) if (mask >> i) & 1]


def _mk(engines):
    m = 0
    for i in engines:
        m |= 1 << i
    return m


def _plan(T, topo):
    cores = list(T.cores)
    cnt = T.tables["CNT"]
    n = len(cores)
    users = [[j for j in range(n) if j != e and cnt[j][e] > 0] for e in range(n)]
    helpers = []
    for e in range(n):
        src = cores[e]
        by_die = {}
        for c in range(NSIM):
            if (topo.host(c), topo.chip(c)) != (topo.host(src), topo.chip(src)) or c in cores:
                continue
            if all(topo.may_write(c, cores[j]) for j in users[e]):
                by_die.setdefault(topo.die(c), []).append(c)
        dies = sorted(by_die, key=lambda d: d != topo.die(src))
        hs = []
        for r in range(len(users[e])):
            for d in dies:
                hs.append(by_die[d][r])
        assert not users[e] or len(hs) in ASSIGN
        helpers.append(hs)
    return cores, cnt, n, users, helpers


def rank_program(g, core, T, topo):
    cores, cnt, n, users, helpers = _plan(T, topo)
    u8 = dt.uint8
    total = [0]

    def slot(j, e):
        return [k for k in range(n) if k != j and cnt[j][k] > 0].index(e)

    def engines_to(e, hcore, j):
        i = users[e].index(j)
        return _bits(topo.mask(hcore, cores[j]))[i::len(users[e])]

    def view(codes_buf, plane_buf, p, o):
        a = o + (p // 2) * TW
        if p % 2 == 0:
            return codes_buf[:, a:a + TW].bitcast(u8)
        return plane_buf[:, a:a + TW]

    rank = T.rank_of(core)

    if rank is None:
        for e in range(n):
            if core not in helpers[e]:
                continue
            me = helpers[e].index(core)
            assign = ASSIGN[len(helpers[e])]
            for p in range(2 * NT):
                if assign[p] != me:
                    continue
                g.wait_ge(T.sem["hp%d" % p], len(_bits(topo.mask(cores[e], core))))
                trs = []
                for j in users[e]:
                    eng = engines_to(e, core, j)
                    rid, pid = topo.addr(cores[j], core)
                    trs.append(RemoteDMATransfer(dst_ids=[DstId(rid=rid, pnc=pid)], dma_engine_mask=_mk(eng),
                                                 remote_sem=T.sem["w%d_%d" % (p // 2, slot(j, e))],
                                                 src=view(T.rc, T.rs, p, 0), dst=view(T.rc, T.rs, p, slot(j, e) * WC)))
                    total[0] += len(eng)
                g.remote_dma_fused(trs, local_sem=T.sem.sent)
            g.wait_ge(T.sem.sent, total[0])
        return

    own, foreign = [], []
    c0 = 0
    for e in range(n):
        m = cnt[rank][e]
        assert m % CH == 0
        for q in range(m // CH):
            (own if e == rank else foreign).append((c0 + q * CH, e))
        c0 += m
    foreign.sort(key=lambda ae: (len(users[ae[1]]), ae[0]))
    groups = [grp for grp in (own, foreign) if grp]
    order = own + foreign

    te, ve, se, sy = g.tensor, g.vector, g.scalar, g.sync

    for t in range(NT):
        src = T.w1[:, 4 * TW * t:4 * TW * (t + 1)] if t < 2 else T.w2[:, :]
        sy.dma_start(T.wt[:, 4 * TW * t:4 * TW * (t + 1)], src).then_inc(T.sem["l%d" % t], 16)
    sy.wait_ge(T.sem.go, 1)
    for k, (a, e) in enumerate(order):
        sy.dma_start(T.xt[:, 4 * a:4 * (a + CH)], T.x[:, 4 * a:4 * (a + CH)]).then_inc(T.sem["lx%d" % k], 16)

    for t in range(NT):
        ve.wait_ge(T.sem["l%d" % t], 16)
        ve.quantize_mx(T.wqc[:, TW * t:TW * (t + 1)], T.wqs[:, TW * t:TW * (t + 1)],
                       T.wt[:, 4 * TW * t:4 * TW * (t + 1)]).then_inc(T.sem["q%d" % t], 1)
    for k, (a, e) in enumerate(order):
        ve.wait_ge(T.sem["lx%d" % k], 16)
        ve.quantize_mx(T.xqc[:, a:a + CH], T.xqs[:, a:a + CH], T.xt[:, 4 * a:4 * (a + CH)]).then_inc(T.sem["xq%d" % k], 1)

    for t in range(NT):
        g.wait_ge(T.sem["q%d" % t], 1)
        if not users[rank]:
            continue
        assign = ASSIGN[len(helpers[rank])]
        for p in (2 * t, 2 * t + 1):
            hcore = helpers[rank][assign[p]]
            rid, pid = topo.addr(hcore, core)
            m = topo.mask(core, hcore)
            g.remote_dma(out_ap=view(T.rc, T.rs, p, 0), in_ap=view(T.wqc, T.wqs, p, 0), remote_sem=T.sem["hp%d" % p],
                         local_sem=T.sem.sent, pid=pid, routing_id=rid, dma_engine_mask=m)
            total[0] += len(_bits(m))
    g.sem_inc(T.sem.go, 1)
    g.wait_ge(T.sem.sent, total[0])

    def weights(e):
        if e == rank:
            return T.wqc, T.wqs, 0
        return T.rc, T.rs, slot(rank, e) * WC

    waited = set()

    def wait_tile(e, t):
        if (e, t) in waited:
            return
        waited.add((e, t))
        if e == rank:
            te.wait_ge(T.sem["q%d" % t], 1)
            return
        assign = ASSIGN[len(helpers[e])]
        cntr = sum(len(engines_to(e, helpers[e][assign[p]], rank)) for p in (2 * t, 2 * t + 1))
        te.wait_ge(T.sem["w%d_%d" % (t, slot(rank, e))], cntr)

    k0 = 0
    nst = 0
    for grp in groups:
        ks = list(range(k0, k0 + len(grp)))
        k0 += len(grp)
        experts = []
        for a, e in grp:
            if e not in experts:
                experts.append(e)
        for e in experts:
            wc, ws, o = weights(e)
            for i, nm in enumerate(("za", "zb")):
                wait_tile(e, i)
                for k, (a, e2) in zip(ks, grp):
                    if e2 != e:
                        continue
                    if i == 0:
                        te.wait_ge(T.sem["xq%d" % k], 1)
                    te.matmul_mx(T.ps[:, 512 * (2 * k + i):512 * (2 * k + i) + CH],
                                 wc[:, o + i * TW:o + (i + 1) * TW], ws[:, o + i * TW:o + (i + 1) * TW],
                                 T.xqc[:, a:a + CH], T.xqs[:, a:a + CH], True, True).then_inc(T.sem["%s%d" % (nm, k)], 1)
        for k, (a, e) in zip(ks, grp):
            wc, ws, o = weights(e)
            wait_tile(e, 2)
            te.wait_ge(T.sem["hq%d" % k], 1)
            te.matmul_mx(T.ps[:, 512 * 2 * k:512 * 2 * k + CH],
                         wc[:, o + 2 * TW:o + 3 * TW], ws[:, o + 2 * TW:o + 3 * TW],
                         T.hqc[:, a:a + CH], T.hqs[:, a:a + CH], True, True).then_inc(T.sem["p%d" % k], 1)

        def quant(k, a):
            ve.wait_ge(T.sem["act%d" % k], 4)
            ve.quantize_mx(T.hqc[:, a:a + CH], T.hqs[:, a:a + CH], T.h[:, 4 * a:4 * (a + CH)]).then_inc(T.sem["hq%d" % k], 1)

        prev = None
        for k, (a, e) in zip(ks, grp):
            z = T.ps[:, 512 * 2 * k:512 * 2 * k + CH]
            ve.wait_ge(T.sem["za%d" % k], 1)
            ve.tensor_scalar(T.h[:, 4 * a + 0:4 * (a + CH):4], z, C, 0.0, AluOpType.mult, AluOpType.max).then_inc(T.sem["act%d" % k], 1)
            ve.tensor_scalar(T.h[:, 4 * a + 1:4 * (a + CH):4], z, -C, 0.0, AluOpType.mult, AluOpType.max).then_inc(T.sem["act%d" % k], 1)
            if prev is not None:
                quant(*prev)
            prev = (k, a)
        quant(*prev)

        for k, (a, e) in zip(ks, grp):
            z = T.ps[:, 512 * (2 * k + 1):512 * (2 * k + 1) + CH]
            se.wait_ge(T.sem["zb%d" % k], 1)
            se.activation(T.h[:, 4 * a + 2:4 * (a + CH):4], z, ActivationFunctionType.Relu, scale=C).then_inc(T.sem["act%d" % k], 1)
            se.activation(T.h[:, 4 * a + 3:4 * (a + CH):4], z, ActivationFunctionType.Relu, scale=-C).then_inc(T.sem["act%d" % k], 1)
        for k, (a, e) in zip(ks, grp):
            se.wait_ge(T.sem["p%d" % k], 1)
            se.activation(T.yo[:, a:a + CH], T.ps[:, 512 * 2 * k:512 * 2 * k + CH], ActivationFunctionType.Copy).then_inc(T.sem["yo%d" % k], 1)

        for k, (a, e) in zip(ks, grp):
            sy.wait_ge(T.sem["yo%d" % k], 1)
            sy.dma_start(T.y[:, a:a + CH], T.yo[:, a:a + CH]).then_inc(T.sem.st, 16)
            nst += 16
    sy.wait_ge(T.sem.st, nst)
